import numpy as np, ml_dtypes
CORES = [3,7,11,15,131,135,139,143]
N = 8
import mx_ref
BF = ml_dtypes.bfloat16
def entries(a):
    return np.ascontiguousarray(a.T).reshape(-1)
def table(e):
    return np.ascontiguousarray(np.reshape(e, (-1, 16)).T).astype(np.int32)
def f(rng, *shape):
    return mx_ref.flush((rng.standard_normal(shape, dtype=np.float32) * np.exp2(rng.integers(-2, 3, shape[:-1] + (1,)))).astype(BF))
def wide(rng, *shape, cols=0):
    v = rng.standard_normal(shape, dtype=np.float32) * np.exp2(rng.integers(-12, 13, shape)).astype(np.float32)
    if cols: v *= np.repeat(np.exp2(rng.integers(-cols, cols + 1, shape[:-2] + (1, shape[-1] // 4))) * (rng.random(shape[:-2] + (1, shape[-1] // 4)) > 0.0625), 4, axis=-1).astype(np.float32)
    return mx_ref.flush(v.astype(BF))
NL, LO, O = 1024, 128, 4
HOST = np.array([0 if k < 128 else 1 for k in CORES])
def tables_of(s):
    return np.stack([table(e) for e in s])
def won(rng, win):
    v = rng.integers(1, 2 ** rng.integers(0, 21, NL) + 1)
    s = rng.integers(0, v, (N, NL)); s[win, np.arange(NL)] = v
    return tables_of(s)
def setup_inputs(rng):
    s = rng.integers(0, 2 ** rng.integers(0, 21, NL) + 1, (N, NL))
    return {"x": f(rng, N, 128, 4 * NL), "w": f(rng, N, 128, 512 * O), "sc": tables_of(s)}
def setup_inputs_ties(rng):
    s = np.zeros((N, NL), int)
    for q in range(N):
        for i, j in enumerate(rng.permutation(LO) + q * LO):
            a, b = [rng.permutation(np.flatnonzero(HOST == h)) for h in rng.permutation(2)]
            if i % 3 == 0: e = np.arange(N)
            elif i % 3 == 1: e = a[:rng.integers(2, len(a) + 1)]
            else: e = np.concatenate([a[:rng.integers(1, len(a) + 1)], b[:rng.integers(1, len(b) + 1)]])
            v = 0 if i == 0 else 2 ** 20 if i < 4 else int(rng.integers(1, 2 ** 20 + 1))
            s[:, j] = rng.integers(0, max(v, 1), N); s[e, j] = v
    return {**setup_inputs(rng), "sc": tables_of(s)}
def setup_inputs_close(rng):
    v = rng.integers(1, 2 ** rng.integers(0, 21, NL) + 1)
    v.reshape(N, LO)[:, rng.permutation(LO)[:2]] = [1, 2 ** 20]
    win = rng.integers(0, N, NL); second = (win + rng.integers(1, N, NL)) % N
    s = np.where(rng.random((N, NL)) < 0.5, v - 1, rng.integers(0, v, (N, NL)))
    s[second, np.arange(NL)] = v - 1; s[win, np.arange(NL)] = v
    return {**setup_inputs(rng), "sc": tables_of(s)}
def setup_inputs_most(rng):
    p = int(rng.integers(0, N))
    win = (p + rng.integers(1, N, (N, LO))) % N
    for i, q in enumerate(rng.permutation(N)):
        if i == 0: win[q] = p
        elif i > 1: win[q, rng.permutation(LO)[:-(-9 * LO // 10)]] = p
    return {**setup_inputs(rng), "sc": won(rng, win.reshape(-1))}
def setup_inputs_sides(rng):
    win = np.zeros((N, LO), int)
    for h in range(2):
        own = rng.permutation(np.flatnonzero(HOST == h))
        for i, q in enumerate(own):
            win[q] = rng.choice(np.flatnonzero(HOST == (1 - h if i < len(own) // 2 else h)), LO)
    return {**setup_inputs(rng), "sc": won(rng, win.reshape(-1))}
def setup_inputs_spread(rng):
    d = setup_inputs(rng); d["x"] = wide(rng, N, 128, 4 * NL, cols=6); return d
def check_inputs(d):
    b = []
    for r in range(N):
        s = entries(d["sc"][r])
        if s.min() < 0 or s.max() > 2 ** 20: b.append("sc")
    return b
def reference(x, w, sc):
    best = np.stack([entries(e) for e in sc]).argmax(axis=0)
    y = np.zeros((N, 128, O * LO), np.float32)
    for q in range(N):
        M = np.concatenate([x[best[l]][:, 4 * l:4 * l + 4] for l in range(q * LO, q * LO + LO)], axis=1)
        M = mx_ref.quantize(M)
        for o in range(O): y[q][:, LO * o:LO * o + LO] = mx_ref.matmul(mx_ref.quantize(w[q][:, 512 * o:512 * o + 512]), M)
    return {"y": y}

@@ -1,0 +1,273 @@
+from concourse.bass import DstId, RemoteDMATransfer
+from concourse.mybir import dt, AluOpType, ActivationFunctionType
+
+C = 128
+KC = C // 16
+
+CODE = "float8_e4m3fn_x4"
+SCRATCH = {
+    "xs": ("sbuf", [128, 4096], "bfloat16"),
+    "ws": ("sbuf", [128, 2048], "bfloat16"),
+    "scs": ("sbuf", [128, 64], "int32"),
+    "keys": ("sbuf", [128, 64], "int32"),
+    "keyland": ("sbuf", [128, 48], "int32"),
+    "max1": ("sbuf", [128, 16], "int32"),
+    "max2": ("sbuf", [128, 16], "int32"),
+    "best": ("sbuf", [128, 16], "int32"),
+    "xkey": ("sbuf", [128, KC], "int32"),
+    "xkeyland": ("sbuf", [128, KC], "int32"),
+    "fin": ("sbuf", [128, KC], "int32"),
+    "pidx": ("sbuf", [128, KC], "int32"),
+    "p16": ("sbuf", [128, KC], "int32"),
+    "c16": ("sbuf", [128, KC], "int32"),
+    "jint": ("sbuf", [128, KC], "int32"),
+    "jfrac": ("sbuf", [128, KC], "float32"),
+    "lowx": ("sbuf", [128, KC], "int32"),
+    "posx": ("sbuf", [128, KC], "float32"),
+    "offx": ("sbuf", [128, KC], "uint16"),
+    "lowf": ("sbuf", [128, KC], "int32"),
+    "posf": ("sbuf", [128, KC], "float32"),
+    "offf": ("sbuf", [128, KC], "uint16"),
+    "qxc": ("sbuf", [128, 4 * C], CODE),
+    "qxs": ("sbuf", [128, 4 * C], "uint8"),
+    "qoc": ("sbuf", [128, 4 * C], CODE),
+    "qos": ("sbuf", [128, 4 * C], "uint8"),
+    "winx": ("sbuf", [128, 4 * C], CODE),
+    "winxs": ("sbuf", [128, 4 * C], "uint8"),
+    "wino": ("sbuf", [128, 5 * C], CODE),
+    "winos": ("sbuf", [128, 5 * C], "uint8"),
+    "selc": ("sbuf", [128, C], CODE),
+    "sels": ("sbuf", [128, C], "uint8"),
+    "mc": ("sbuf", [128, C], CODE),
+    "ms": ("sbuf", [128, C], "uint8"),
+    "wc": ("sbuf", [128, 512], CODE),
+    "wsc": ("sbuf", [128, 512], "uint8"),
+    "ps": ("psum", [128, 2048], "float32"),
+    "ysb": ("sbuf", [128, 512], "float32"),
+}
+SEMAPHORES = [
+    "ld_xa", "ld_xn", "ld_o", "ld_w", "ld_sc",
+    "iot", "b0", "b1", "b2", "kmade", "qx", "qxo", "qo", "qoo", "qw",
+    "mx12", "mx3", "lx0", "lx1", "lx2", "ck", "f0", "f1", "f2", "f3",
+    "pkxc", "pkxs", "pkfc", "pkfs",
+    "a_key", "a_xc", "a_xs", "a_oc", "a_os", "a_ck", "a_cc", "a_cs", "left",
+    "mm0", "mm1", "mm2", "mm3", "cp0", "cp1", "cp2", "cp3", "st0", "st1",
+]
+
+
+def mask_of(engines):
+    m = 0
+    for e in engines:
+        m |= 1 << e
+    return m
+
+
+def rank_program(g, core, T, topo):
+    rank = T.rank_of(core)
+    if rank is None:
+        return
+    cores = list(T.cores)
+    n = len(cores)
+    mine = [r for r in range(n) if topo.host(cores[r]) == topo.host(core)]
+    others = [r for r in range(n) if r not in mine]
+    pos = mine.index(rank)
+    partner = cores[others[pos]]
+    first = mine[0] < others[0]
+    peers = [p for p in range(len(mine)) if p != pos]
+    away = [p for p in peers if topo.chip(cores[mine[p]]) != topo.chip(core)]
+    near = [p for p in peers if p not in away]
+    V, S, P, D = g.vector, g.scalar, g.tensor, g.sync
+    sem = T.sem
+    A = AluOpType
+
+    t0 = 1 if first else 0
+    xadd = 4 if first else 0
+
+    def xslot(p):
+        return len(mine) - 1 - p
+
+    def oslot(p):
+        return xslot(p) + t0
+
+    def split(pp):
+        c = cores[mine[pp]]
+        ps = [p for p in range(len(mine)) if p != pp]
+        aw = [p for p in ps if topo.chip(cores[mine[p]]) != topo.chip(c)]
+        off = topo.engines(c, cores[mine[aw[0]]])
+        k = len(off) // len(aw)
+        m = {}
+        for i, p in enumerate(aw):
+            m[p] = off[i * k:(i + 1) * k]
+        for p in ps:
+            if p not in aw:
+                rest = [e for e in topo.engines(c, cores[mine[p]]) if e not in off]
+                m[p] = rest[::len(rest) // k]
+        return m
+
+    masks = split(pos)
+    arr = 0
+    for p in peers:
+        arr += len(split(p)[pos])
+    sent = [0]
+
+    def spread(remote_sem, src, dst):
+        tr = []
+        for p in peers:
+            rid, pid = topo.addr(cores[mine[p]], core)
+            tr.append(RemoteDMATransfer(dst_ids=[DstId(rid=rid, pnc=pid)], dma_engine_mask=mask_of(masks[p]),
+                                        remote_sem=remote_sem, srcs=[src(p)], dsts=[dst(p)]))
+            sent[0] += len(masks[p])
+        g.remote_dma_fused(tr, local_sem=sem.left)
+
+    far_in = len(topo.engines(partner, core))
+
+    def cross(out, in_, remote_sem):
+        rid, pid = topo.addr(partner, core)
+        g.remote_dma(out, in_, remote_sem, sem.left, pid, rid, topo.mask(core, partner))
+        sent[0] += len(topo.engines(core, partner))
+
+    def load_x(ranks, s):
+        a, b = 4 * C * min(ranks), 4 * C * (max(ranks) + 1)
+        D.dma_start(T.xs[:, a:b], T.x[:, a:b]).then_inc(s, 16)
+
+    load_x([others[p] for p in away], sem.ld_xa)
+    for k in range(8):
+        (D if k < 4 else S).dma_start(T.scs[16 * k:16 * k + 16, :], T.sc[:]).then_inc(sem.ld_sc, 16)
+    load_x([others[p] for p in near + [pos]], sem.ld_xn)
+    load_x(mine, sem.ld_o)
+    D.dma_start(T.ws[:], T.w[:]).then_inc(sem.ld_w, 16)
+
+    g.iota(T.pidx[:], [[0, KC]], 0, 1).then_inc(sem.iot, 1)
+    g.iota(T.c16[:], [[16, KC]], 0, 0).then_inc(sem.iot, 1)
+    V.wait_ge(sem.iot, 2)
+    V.tensor_scalar(T.p16[:], T.pidx[:], 15, None, A.bitwise_and).then_inc(sem.b0, 1)
+    V.wait_ge(sem.b0, 1)
+    V.tensor_tensor(T.jint[:], T.p16[:], T.c16[:], A.add).then_inc(sem.b1, 1)
+    V.wait_ge(sem.b1, 1)
+    V.tensor_scalar(T.jfrac[:], T.jint[:], 1.0 / C, None, A.mult).then_inc(sem.b2, 1)
+
+    nb = KC * len(mine)
+    V.wait_ge(sem.ld_sc, 128)
+    V.tensor_scalar(T.keys[:, 0:2 * nb:2], T.scs[:, KC * mine[0]:KC * mine[0] + nb], 8.0, float(oslot(pos)),
+                    A.mult, A.add).then_inc(sem.kmade, 1)
+    V.tensor_scalar(T.keys[:, 1:2 * nb:2], T.scs[:, KC * others[0]:KC * others[0] + nb], 8.0, float(xslot(pos) + xadd),
+                    A.mult, A.add).then_inc(sem.kmade, 1)
+    g.wait_ge(sem.kmade, 2)
+
+    def lane(me, to):
+        return me if me < to else me - 1
+
+    spread(sem.a_key, lambda p: T.keys[:, 2 * KC * p:2 * KC * (p + 1)],
+           lambda p: T.keyland[:, 2 * KC * lane(pos, p):2 * KC * (lane(pos, p) + 1)])
+
+    def runs(ps):
+        out = []
+        for p in sorted(ps):
+            if out and out[-1][1] == p:
+                out[-1][1] = p + 1
+            else:
+                out.append([p, p + 1])
+        return out
+
+    def quant(codes, scales, ranks, lo, hi, s):
+        V.quantize_mx(codes, scales, T.xs[:, 4 * C * ranks[lo]:4 * C * (ranks[hi - 1] + 1)]).then_inc(s, 1)
+
+    ax = C * xslot(pos)
+    ao = C * oslot(pos)
+    V.wait_ge(sem.ld_xa, 16)
+    for u, v in runs(away):
+        quant(T.qxc[:, C * u:C * v], T.qxs[:, C * u:C * v], others, u, v, sem.qx)
+    V.wait_ge(sem.ld_xn, 16)
+    for u, v in runs(near):
+        quant(T.qxc[:, C * u:C * v], T.qxs[:, C * u:C * v], others, u, v, sem.qx)
+    quant(T.winx[:, ax:ax + C], T.winxs[:, ax:ax + C], others, pos, pos + 1, sem.qxo)
+    V.wait_ge(sem.ld_o, 16)
+    for u, v in runs(peers):
+        quant(T.qoc[:, C * u:C * v], T.qos[:, C * u:C * v], mine, u, v, sem.qo)
+    quant(T.wino[:, ao:ao + C], T.winos[:, ao:ao + C], mine, pos, pos + 1, sem.qoo)
+
+    g.wait_ge(sem.qx, len(runs(away)) + len(runs(near)))
+    spread(sem.a_xc, lambda p: T.qxc[:, C * p:C * (p + 1)].bitcast(dt.uint8), lambda p: T.winx[:, ax:ax + C].bitcast(dt.uint8))
+    spread(sem.a_xs, lambda p: T.qxs[:, C * p:C * (p + 1)], lambda p: T.winxs[:, ax:ax + C])
+    g.wait_ge(sem.qo, len(runs(peers)))
+    spread(sem.a_oc, lambda p: T.qoc[:, C * p:C * (p + 1)].bitcast(dt.uint8), lambda p: T.wino[:, ao:ao + C].bitcast(dt.uint8))
+    spread(sem.a_os, lambda p: T.qos[:, C * p:C * (p + 1)], lambda p: T.winos[:, ao:ao + C])
+
+    V.wait_ge(sem.a_key, arr)
+    V.tensor_tensor(T.max1[:], T.keyland[:, 0:2 * KC], T.keyland[:, 2 * KC:4 * KC], A.max).then_inc(sem.mx12, 1)
+    V.wait_ge(sem.kmade, 2)
+    V.tensor_tensor(T.max2[:], T.keyland[:, 4 * KC:6 * KC], T.keys[:, 2 * KC * pos:2 * KC * (pos + 1)],
+                    A.max).then_inc(sem.mx12, 1)
+    V.wait_ge(sem.mx12, 2)
+    V.tensor_tensor(T.best[:], T.max1[:], T.max2[:], A.max).then_inc(sem.mx3, 1)
+    V.wait_ge(sem.mx3, 1)
+    V.tensor_scalar(T.lowx[:], T.best[:, 1:2 * KC:2], 7, None, A.bitwise_and).then_inc(sem.lx0, 1)
+    V.tensor_scalar(T.xkey[:], T.best[:, 1:2 * KC:2], 0x7FFFFFFC, None, A.bitwise_and).then_inc(sem.ck, 1)
+    V.wait_ge(sem.lx0, 1)
+    V.wait_ge(sem.b2, 1)
+    V.tensor_tensor(T.posx[:], T.lowx[:], T.jfrac[:], A.add).then_inc(sem.lx1, 1)
+    V.wait_ge(sem.lx1, 1)
+    V.tensor_scalar(T.offx[:], T.posx[:], float(C), float(-C * xadd), A.mult, A.add).then_inc(sem.lx2, 1)
+    g.wait_ge(sem.ck, 1)
+    cross(T.xkeyland[:], T.xkey[:], sem.a_ck)
+
+    V.wait_ge(sem.lx2, 1)
+    V.wait_ge(sem.qxo, 1)
+    V.wait_ge(sem.a_xc, arr)
+    V.tensor_copy(T.selc[:].bitcast(dt.uint32),
+                  T.winx[:].bitcast(dt.uint32).indirect(T.offx[:, 0:KC])).then_inc(sem.pkxc, 1)
+    S.wait_ge(sem.lx2, 1)
+    S.wait_ge(sem.qxo, 1)
+    S.wait_ge(sem.a_xs, arr)
+    S.activation(T.sels[:], T.winxs[:].indirect(T.offx[:, 0:KC]), ActivationFunctionType.Copy).then_inc(sem.pkxs, 1)
+    b = C * xadd
+    g.wait_ge(sem.pkxc, 1)
+    cross(T.wino[:, b:b + C].bitcast(dt.uint8), T.selc[:].bitcast(dt.uint8), sem.a_cc)
+    g.wait_ge(sem.pkxs, 1)
+    cross(T.winos[:, b:b + C], T.sels[:], sem.a_cs)
+
+    V.wait_ge(sem.ld_w, 16)
+    V.quantize_mx(T.wc[:], T.wsc[:], T.ws[:]).then_inc(sem.qw, 1)
+
+    V.wait_ge(sem.a_ck, far_in)
+    V.tensor_tensor(T.fin[:], T.best[:, 0:2 * KC:2], T.xkeyland[:], A.max).then_inc(sem.f0, 1)
+    V.wait_ge(sem.f0, 1)
+    V.tensor_scalar(T.lowf[:], T.fin[:], 7, None, A.bitwise_and).then_inc(sem.f1, 1)
+    V.wait_ge(sem.f1, 1)
+    V.tensor_tensor(T.posf[:], T.lowf[:], T.jfrac[:], A.add).then_inc(sem.f2, 1)
+    V.wait_ge(sem.f2, 1)
+    V.tensor_scalar(T.offf[:], T.posf[:], float(C), None, A.mult).then_inc(sem.f3, 1)
+    V.wait_ge(sem.f3, 1)
+    V.wait_ge(sem.qoo, 1)
+    V.wait_ge(sem.a_oc, arr)
+    V.wait_ge(sem.a_cc, far_in)
+    V.tensor_copy(T.mc[:].bitcast(dt.uint32),
+                  T.wino[:].bitcast(dt.uint32).indirect(T.offf[:, 0:KC])).then_inc(sem.pkfc, 1)
+    S.wait_ge(sem.f3, 1)
+    S.wait_ge(sem.qoo, 1)
+    S.wait_ge(sem.a_os, arr)
+    S.wait_ge(sem.a_cs, far_in)
+    S.activation(T.ms[:], T.winos[:].indirect(T.offf[:, 0:KC]), ActivationFunctionType.Copy).then_inc(sem.pkfs, 1)
+
+    P.wait_ge(sem.qw, 1)
+    P.wait_ge(sem.pkfc, 1)
+    P.wait_ge(sem.pkfs, 1)
+    for o in range(4):
+        P.matmul_mx(T.ps[:, 512 * o:512 * o + C], T.wc[:, C * o:C * (o + 1)], T.wsc[:, C * o:C * (o + 1)],
+                    T.mc[:], T.ms[:], True, True).then_inc(sem["mm%d" % o], 1)
+    for o in (0, 2):
+        V.wait_ge(sem["mm%d" % o], 1)
+        V.tensor_copy(T.ysb[:, C * o:C * (o + 1)], T.ps[:, 512 * o:512 * o + C]).then_inc(sem["cp%d" % o], 1)
+    for o in (1, 3):
+        S.wait_ge(sem["mm%d" % o], 1)
+        S.activation(T.ysb[:, C * o:C * (o + 1)], T.ps[:, 512 * o:512 * o + C],
+                     ActivationFunctionType.Copy).then_inc(sem["cp%d" % o], 1)
+    D.wait_ge(sem.cp0, 1)
+    D.wait_ge(sem.cp1, 1)
+    D.dma_start(T.y[:, 0:2 * C], T.ysb[:, 0:2 * C]).then_inc(sem.st0, 16)
+    S.wait_ge(sem.cp2, 1)
+    S.wait_ge(sem.cp3, 1)
+    S.dma_start(T.y[:, 2 * C:4 * C], T.ysb[:, 2 * C:4 * C]).then_inc(sem.st1, 16)
+    D.wait_ge(sem.st0, 16)
+    S.wait_ge(sem.st1, 16)
+    g.wait_ge(sem.left, sent[0])

@@ -3,17 +3,18 @@ from concourse.mybir import dt, AluOpType, ActivationFunctionType
 
 C = 128
 KC = C // 16
+HALF = 64
 
 CODE = "float8_e4m3fn_x4"
 SCRATCH = {
     "xs": ("sbuf", [128, 4096], "bfloat16"),
     "ws": ("sbuf", [128, 2048], "bfloat16"),
     "scs": ("sbuf", [128, 64], "int32"),
-    "keys": ("sbuf", [128, 64], "int32"),
-    "keyland": ("sbuf", [128, 48], "int32"),
-    "max1": ("sbuf", [128, 16], "int32"),
-    "max2": ("sbuf", [128, 16], "int32"),
-    "best": ("sbuf", [128, 16], "int32"),
+    "keys": ("sbuf", [128, 4 * KC], "int32"),
+    "keyland": ("sbuf", [128, 3 * KC], "int32"),
+    "max1": ("sbuf", [128, KC], "int32"),
+    "max2": ("sbuf", [128, KC], "int32"),
+    "best": ("sbuf", [128, KC], "int32"),
     "xkey": ("sbuf", [128, KC], "int32"),
     "xkeyland": ("sbuf", [128, KC], "int32"),
     "fin": ("sbuf", [128, KC], "int32"),
@@ -32,6 +33,7 @@ SCRATCH = {
     "qxs": ("sbuf", [128, 4 * C], "uint8"),
     "qoc": ("sbuf", [128, 4 * C], CODE),
     "qos": ("sbuf", [128, 4 * C], "uint8"),
+    "relc": ("sbuf", [128, 2 * C], CODE),
     "winx": ("sbuf", [128, 4 * C], CODE),
     "winxs": ("sbuf", [128, 4 * C], "uint8"),
     "wino": ("sbuf", [128, 5 * C], CODE),
@@ -46,11 +48,11 @@ SCRATCH = {
     "ysb": ("sbuf", [128, 512], "float32"),
 }
 SEMAPHORES = [
-    "ld_xa", "ld_xn", "ld_o", "ld_w", "ld_sc",
-    "iot", "b0", "b1", "b2", "kmade", "qx", "qxo", "qo", "qoo", "qw",
+    "ld_xa", "ld_xn", "ld_oa", "ld_on", "ld_w0", "ld_w1", "ld_sc", "xsent",
+    "iot", "b0", "b1", "b2", "kmade", "qx", "qxo", "qoa", "qon", "qoo", "qw0", "qw1",
     "mx12", "mx3", "lx0", "lx1", "lx2", "ck", "f0", "f1", "f2", "f3",
     "pkxc", "pkxs", "pkfc", "pkfs",
-    "a_key", "a_xc", "a_xs", "a_oc", "a_os", "a_ck", "a_cc", "a_cs", "left",
+    "a_key", "a_rc", "a_xc", "a_xs", "a_oc", "a_os", "a_ck", "a_cc", "a_cs", "left",
     "mm0", "mm1", "mm2", "mm3", "cp0", "cp1", "cp2", "cp3", "st0", "st1",
 ]
 
@@ -62,11 +64,59 @@ def mask_of(engines):
     return m
 
 
+def helper_of(c, cores, topo):
+    host = [k for k in cores if topo.host(k) == topo.host(c)]
+    return [h for h in topo.cores_of(c)
+            if h not in cores and topo.die(h) == topo.die(c) and all(topo.may_write(h, k) for k in host)][0]
+
+
+def split(src, dsts, topo, wide=True):
+    aw = [d for d in dsts if d not in topo.cores_of(src)]
+    off = topo.engines(src, aw[0])
+    k = len(off) // len(aw)
+    m = {}
+    for i, d in enumerate(aw):
+        m[d] = off[i * k:(i + 1) * k]
+    for d in dsts:
+        if d not in aw:
+            rest = [e for e in topo.engines(src, d) if e not in off]
+            m[d] = rest if wide else rest[::len(rest) // k]
+    return m
+
+
+def fused(g, topo, core, masks, local_sem, sides):
+    tr = []
+    for d, s, src, dst in sides:
+        rid, pid = topo.addr(d, core)
+        tr.append(RemoteDMATransfer(dst_ids=[DstId(rid=rid, pnc=pid)], dma_engine_mask=mask_of(masks[d]),
+                                    remote_sem=s, srcs=[src], dsts=[dst]))
+    g.remote_dma_fused(tr, local_sem=local_sem)
+    return sum(len(masks[d]) for d in masks)
+
+
+def u8(view):
+    return view.bitcast(dt.uint8)
+
+
+def helper_program(g, core, boss, T, topo):
+    cores = list(T.cores)
+    mine = [c for c in cores if topo.host(c) == topo.host(boss)]
+    away = [c for c in mine if c not in topo.cores_of(boss)]
+    ao = C * (len(mine) - 1 - mine.index(boss) + (1 if mine[0] == cores[0] else 0))
+    g.wait_ge(T.sem.a_rc, len(split(boss, away + [core], topo)[core]))
+    sent = fused(g, topo, core, split(core, away, topo), T.sem.left,
+                 [(d, T.sem.a_oc, u8(T.relc[:, C * i:C * (i + 1)]), u8(T.wino[:, ao:ao + C])) for i, d in enumerate(away)])
+    g.wait_ge(T.sem.left, sent)
+
+
 def rank_program(g, core, T, topo):
     rank = T.rank_of(core)
-    if rank is None:
-        return
     cores = list(T.cores)
+    if rank is None:
+        for c in cores:
+            if helper_of(c, cores, topo) == core:
+                helper_program(g, core, c, T, topo)
+        return
     n = len(cores)
     mine = [r for r in range(n) if topo.host(cores[r]) == topo.host(core)]
     others = [r for r in range(n) if r not in mine]
@@ -75,199 +125,179 @@ def rank_program(g, core, T, topo):
     first = mine[0] < others[0]
     peers = [p for p in range(len(mine)) if p != pos]
     away = [p for p in peers if topo.chip(cores[mine[p]]) != topo.chip(core)]
-    near = [p for p in peers if p not in away]
+    near = [p for p in peers if p not in away][0]
+    host = [cores[r] for r in mine]
+    helper = helper_of(core, cores, topo)
     V, S, P, D = g.vector, g.scalar, g.tensor, g.sync
     sem = T.sem
     A = AluOpType
 
-    t0 = 1 if first else 0
     xadd = 4 if first else 0
+    xslot = len(mine) - 1 - pos
+    oslot = xslot + (1 if first else 0)
+    ax, ao, ap = C * xslot, C * oslot, C * xadd
 
-    def xslot(p):
-        return len(mine) - 1 - p
+    def but(c):
+        return [k for k in host if k != c]
 
-    def oslot(p):
-        return xslot(p) + t0
-
-    def split(pp):
-        c = cores[mine[pp]]
-        ps = [p for p in range(len(mine)) if p != pp]
-        aw = [p for p in ps if topo.chip(cores[mine[p]]) != topo.chip(c)]
-        off = topo.engines(c, cores[mine[aw[0]]])
-        k = len(off) // len(aw)
-        m = {}
-        for i, p in enumerate(aw):
-            m[p] = off[i * k:(i + 1) * k]
-        for p in ps:
-            if p not in aw:
-                rest = [e for e in topo.engines(c, cores[mine[p]]) if e not in off]
-                m[p] = rest[::len(rest) // k]
-        return m
-
-    masks = split(pos)
-    arr = 0
-    for p in peers:
-        arr += len(split(p)[pos])
+    thin = split(core, but(core), topo, False)
+    wide = split(core, but(core), topo)
+    arr_k = sum(len(split(c, but(c), topo, False)[core]) for c in but(core))
+    arr = sum(len(split(c, but(c), topo)[core]) for c in but(core))
+    far_in = len(topo.engines(partner, core))
     sent = [0]
 
-    def spread(remote_sem, src, dst):
-        tr = []
-        for p in peers:
-            rid, pid = topo.addr(cores[mine[p]], core)
-            tr.append(RemoteDMATransfer(dst_ids=[DstId(rid=rid, pnc=pid)], dma_engine_mask=mask_of(masks[p]),
-                                        remote_sem=remote_sem, srcs=[src(p)], dsts=[dst(p)]))
-            sent[0] += len(masks[p])
-        g.remote_dma_fused(tr, local_sem=sem.left)
+    def send(masks, sides):
+        sent[0] += fused(g, topo, core, {d: masks[d] for d, _, _, _ in sides}, sem.left, sides)
 
-    far_in = len(topo.engines(partner, core))
+    def spread(masks, s, src, dst):
+        send(masks, [(host[p], s, src(p), dst(p)) for p in peers])
 
-    def cross(out, in_, remote_sem):
-        rid, pid = topo.addr(partner, core)
-        g.remote_dma(out, in_, remote_sem, sem.left, pid, rid, topo.mask(core, partner))
-        sent[0] += len(topo.engines(core, partner))
+    def block(buf, p, k=1):
+        return buf[:, C * p:C * (p + k)]
 
     def load_x(ranks, s):
         a, b = 4 * C * min(ranks), 4 * C * (max(ranks) + 1)
         D.dma_start(T.xs[:, a:b], T.x[:, a:b]).then_inc(s, 16)
 
+    for k, q in enumerate((D, S)):
+        q.dma_start(T.scs[16 * k:16 * k + 16, :], T.sc[:]).then_inc(sem.ld_sc, 16)
+    load_x([mine[p] for p in away], sem.ld_oa)
     load_x([others[p] for p in away], sem.ld_xa)
-    for k in range(8):
-        (D if k < 4 else S).dma_start(T.scs[16 * k:16 * k + 16, :], T.sc[:]).then_inc(sem.ld_sc, 16)
-    load_x([others[p] for p in near + [pos]], sem.ld_xn)
-    load_x(mine, sem.ld_o)
-    D.dma_start(T.ws[:], T.w[:]).then_inc(sem.ld_w, 16)
+    load_x([others[near], others[pos]], sem.ld_xn)
+    load_x([mine[near], mine[pos]], sem.ld_on)
+    D.dma_start(T.ws[:, 0:1024], T.w[:, 0:1024]).then_inc(sem.ld_w0, 16)
+    D.wait_ge(sem.xsent, 1)
+    D.dma_start(T.ws[:, 1024:2048], T.w[:, 1024:2048]).then_inc(sem.ld_w1, 16)
 
     g.iota(T.pidx[:], [[0, KC]], 0, 1).then_inc(sem.iot, 1)
     g.iota(T.c16[:], [[16, KC]], 0, 0).then_inc(sem.iot, 1)
     V.wait_ge(sem.iot, 2)
     V.tensor_scalar(T.p16[:], T.pidx[:], 15, None, A.bitwise_and).then_inc(sem.b0, 1)
+
+    lo, hi = slice(0, HALF), slice(HALF, 128)
+    nb = KC * len(mine)
+    V.wait_ge(sem.ld_sc, 32)
+    for a in range(0, 128, 32):
+        r0, low = (mine[0], oslot) if a < HALF else (others[0], xslot + xadd)
+        V.tensor_scalar(T.keys[a:a + 32, :], T.scs[0:32, KC * r0:KC * r0 + nb], 8.0, float(low),
+                        A.mult, A.add).then_inc(sem.kmade, 1)
+    g.wait_ge(sem.kmade, 4)
     V.wait_ge(sem.b0, 1)
     V.tensor_tensor(T.jint[:], T.p16[:], T.c16[:], A.add).then_inc(sem.b1, 1)
+
+    def lane(to):
+        return pos if pos < to else pos - 1
+
+    spread(thin, sem.a_key, lambda p: T.keys[:, KC * p:KC * (p + 1)],
+           lambda p: T.keyland[:, KC * lane(p):KC * (lane(p) + 1)])
+
+    def quant(codes, scales, at, ranks, p, k, s):
+        V.quantize_mx(codes[:, at:at + k * C], scales[:, at:at + k * C],
+                      T.xs[:, 4 * C * ranks[p]:4 * C * (ranks[p] + k)]).then_inc(s, 1)
+
+    a0 = min(away)
+    V.wait_ge(sem.ld_oa, 16)
+    quant(T.qoc, T.qos, C * a0, mine, a0, len(away), sem.qoa)
     V.wait_ge(sem.b1, 1)
     V.tensor_scalar(T.jfrac[:], T.jint[:], 1.0 / C, None, A.mult).then_inc(sem.b2, 1)
-
-    nb = KC * len(mine)
-    V.wait_ge(sem.ld_sc, 128)
-    V.tensor_scalar(T.keys[:, 0:2 * nb:2], T.scs[:, KC * mine[0]:KC * mine[0] + nb], 8.0, float(oslot(pos)),
-                    A.mult, A.add).then_inc(sem.kmade, 1)
-    V.tensor_scalar(T.keys[:, 1:2 * nb:2], T.scs[:, KC * others[0]:KC * others[0] + nb], 8.0, float(xslot(pos) + xadd),
-                    A.mult, A.add).then_inc(sem.kmade, 1)
-    g.wait_ge(sem.kmade, 2)
-
-    def lane(me, to):
-        return me if me < to else me - 1
-
-    spread(sem.a_key, lambda p: T.keys[:, 2 * KC * p:2 * KC * (p + 1)],
-           lambda p: T.keyland[:, 2 * KC * lane(pos, p):2 * KC * (lane(pos, p) + 1)])
-
-    def runs(ps):
-        out = []
-        for p in sorted(ps):
-            if out and out[-1][1] == p:
-                out[-1][1] = p + 1
-            else:
-                out.append([p, p + 1])
-        return out
-
-    def quant(codes, scales, ranks, lo, hi, s):
-        V.quantize_mx(codes, scales, T.xs[:, 4 * C * ranks[lo]:4 * C * (ranks[hi - 1] + 1)]).then_inc(s, 1)
-
-    ax = C * xslot(pos)
-    ao = C * oslot(pos)
     V.wait_ge(sem.ld_xa, 16)
-    for u, v in runs(away):
-        quant(T.qxc[:, C * u:C * v], T.qxs[:, C * u:C * v], others, u, v, sem.qx)
+    quant(T.qxc, T.qxs, C * a0, others, a0, len(away), sem.qx)
     V.wait_ge(sem.ld_xn, 16)
-    for u, v in runs(near):
-        quant(T.qxc[:, C * u:C * v], T.qxs[:, C * u:C * v], others, u, v, sem.qx)
-    quant(T.winx[:, ax:ax + C], T.winxs[:, ax:ax + C], others, pos, pos + 1, sem.qxo)
-    V.wait_ge(sem.ld_o, 16)
-    for u, v in runs(peers):
-        quant(T.qoc[:, C * u:C * v], T.qos[:, C * u:C * v], mine, u, v, sem.qo)
-    quant(T.wino[:, ao:ao + C], T.winos[:, ao:ao + C], mine, pos, pos + 1, sem.qoo)
+    quant(T.qxc, T.qxs, C * near, others, near, 1, sem.qx)
+    quant(T.winx, T.winxs, ax, others, pos, 1, sem.qxo)
+    V.wait_ge(sem.ld_on, 16)
+    quant(T.qoc, T.qos, C * near, mine, near, 1, sem.qon)
+    quant(T.wino, T.winos, ao, mine, pos, 1, sem.qoo)
 
-    g.wait_ge(sem.qx, len(runs(away)) + len(runs(near)))
-    spread(sem.a_xc, lambda p: T.qxc[:, C * p:C * (p + 1)].bitcast(dt.uint8), lambda p: T.winx[:, ax:ax + C].bitcast(dt.uint8))
-    spread(sem.a_xs, lambda p: T.qxs[:, C * p:C * (p + 1)], lambda p: T.winxs[:, ax:ax + C])
-    g.wait_ge(sem.qo, len(runs(peers)))
-    spread(sem.a_oc, lambda p: T.qoc[:, C * p:C * (p + 1)].bitcast(dt.uint8), lambda p: T.wino[:, ao:ao + C].bitcast(dt.uint8))
-    spread(sem.a_os, lambda p: T.qos[:, C * p:C * (p + 1)], lambda p: T.winos[:, ao:ao + C])
+    g.wait_ge(sem.qoa, 1)
+    send({helper: wide[host[near]]}, [(helper, sem.a_rc, u8(block(T.qoc, a0, len(away))), u8(T.relc[:]))])
+    g.wait_ge(sem.qx, 2)
+    spread(wide, sem.a_xc, lambda p: u8(block(T.qxc, p)), lambda p: u8(T.winx[:, ax:ax + C]))
+    spread(wide, sem.a_xs, lambda p: block(T.qxs, p), lambda p: T.winxs[:, ax:ax + C])
+    g.wait_ge(sem.qon, 1)
+    spread(wide, sem.a_os, lambda p: block(T.qos, p), lambda p: T.winos[:, ao:ao + C])
+    g.sem_inc(sem.xsent, 1)
 
-    V.wait_ge(sem.a_key, arr)
-    V.tensor_tensor(T.max1[:], T.keyland[:, 0:2 * KC], T.keyland[:, 2 * KC:4 * KC], A.max).then_inc(sem.mx12, 1)
-    V.wait_ge(sem.kmade, 2)
-    V.tensor_tensor(T.max2[:], T.keyland[:, 4 * KC:6 * KC], T.keys[:, 2 * KC * pos:2 * KC * (pos + 1)],
-                    A.max).then_inc(sem.mx12, 1)
+    V.wait_ge(sem.a_key, arr_k)
+    V.tensor_tensor(T.max1[:], T.keyland[:, 0:KC], T.keyland[:, KC:2 * KC], A.max).then_inc(sem.mx12, 1)
+    V.wait_ge(sem.kmade, 4)
+    V.tensor_tensor(T.max2[:], T.keyland[:, 2 * KC:3 * KC], T.keys[:, KC * pos:KC * (pos + 1)], A.max).then_inc(sem.mx12, 1)
     V.wait_ge(sem.mx12, 2)
     V.tensor_tensor(T.best[:], T.max1[:], T.max2[:], A.max).then_inc(sem.mx3, 1)
     V.wait_ge(sem.mx3, 1)
-    V.tensor_scalar(T.lowx[:], T.best[:, 1:2 * KC:2], 7, None, A.bitwise_and).then_inc(sem.lx0, 1)
-    V.tensor_scalar(T.xkey[:], T.best[:, 1:2 * KC:2], 0x7FFFFFFC, None, A.bitwise_and).then_inc(sem.ck, 1)
+    V.tensor_scalar(T.lowx[hi, :], T.best[hi, :], 7, None, A.bitwise_and).then_inc(sem.lx0, 1)
+    V.tensor_scalar(T.xkey[:], T.best[:], 0x7FFFFFFC, None, A.bitwise_and).then_inc(sem.ck, 1)
     V.wait_ge(sem.lx0, 1)
     V.wait_ge(sem.b2, 1)
-    V.tensor_tensor(T.posx[:], T.lowx[:], T.jfrac[:], A.add).then_inc(sem.lx1, 1)
+    V.tensor_tensor(T.posx[hi, :], T.lowx[hi, :], T.jfrac[hi, :], A.add).then_inc(sem.lx1, 1)
     V.wait_ge(sem.lx1, 1)
-    V.tensor_scalar(T.offx[:], T.posx[:], float(C), float(-C * xadd), A.mult, A.add).then_inc(sem.lx2, 1)
+    for half in (lo, hi):
+        V.tensor_scalar(T.offx[half, :], T.posx[hi, :], float(C), float(-C * xadd), A.mult, A.add).then_inc(sem.lx2, 1)
+    last = split(core, [partner, host[near]], topo)
     g.wait_ge(sem.ck, 1)
-    cross(T.xkeyland[:], T.xkey[:], sem.a_ck)
+    send(last, [(partner, sem.a_ck, T.xkey[:], T.xkeyland[:])])
 
-    V.wait_ge(sem.lx2, 1)
+    V.wait_ge(sem.lx2, 2)
     V.wait_ge(sem.qxo, 1)
     V.wait_ge(sem.a_xc, arr)
     V.tensor_copy(T.selc[:].bitcast(dt.uint32),
                   T.winx[:].bitcast(dt.uint32).indirect(T.offx[:, 0:KC])).then_inc(sem.pkxc, 1)
-    S.wait_ge(sem.lx2, 1)
+    S.wait_ge(sem.lx2, 2)
     S.wait_ge(sem.qxo, 1)
     S.wait_ge(sem.a_xs, arr)
     S.activation(T.sels[:], T.winxs[:].indirect(T.offx[:, 0:KC]), ActivationFunctionType.Copy).then_inc(sem.pkxs, 1)
-    b = C * xadd
     g.wait_ge(sem.pkxc, 1)
-    cross(T.wino[:, b:b + C].bitcast(dt.uint8), T.selc[:].bitcast(dt.uint8), sem.a_cc)
+    send(last, [(partner, sem.a_cc, u8(T.selc[:]), u8(T.wino[:, ap:ap + C])),
+                (host[near], sem.a_oc, u8(block(T.qoc, near)), u8(T.wino[:, ao:ao + C]))])
     g.wait_ge(sem.pkxs, 1)
-    cross(T.winos[:, b:b + C], T.sels[:], sem.a_cs)
+    send(last, [(partner, sem.a_cs, T.sels[:], T.winos[:, ap:ap + C])])
 
-    V.wait_ge(sem.ld_w, 16)
-    V.quantize_mx(T.wc[:], T.wsc[:], T.ws[:]).then_inc(sem.qw, 1)
-
+    V.wait_ge(sem.ld_w0, 16)
+    V.quantize_mx(T.wc[:, 0:256], T.wsc[:, 0:256], T.ws[:, 0:1024]).then_inc(sem.qw0, 1)
     V.wait_ge(sem.a_ck, far_in)
-    V.tensor_tensor(T.fin[:], T.best[:, 0:2 * KC:2], T.xkeyland[:], A.max).then_inc(sem.f0, 1)
+    V.tensor_tensor(T.fin[lo, :], T.best[lo, :], T.xkeyland[hi, :], A.max).then_inc(sem.f0, 1)
     V.wait_ge(sem.f0, 1)
-    V.tensor_scalar(T.lowf[:], T.fin[:], 7, None, A.bitwise_and).then_inc(sem.f1, 1)
+    V.tensor_scalar(T.lowf[lo, :], T.fin[lo, :], 7, None, A.bitwise_and).then_inc(sem.f1, 1)
     V.wait_ge(sem.f1, 1)
-    V.tensor_tensor(T.posf[:], T.lowf[:], T.jfrac[:], A.add).then_inc(sem.f2, 1)
+    V.tensor_tensor(T.posf[lo, :], T.lowf[lo, :], T.jfrac[lo, :], A.add).then_inc(sem.f2, 1)
     V.wait_ge(sem.f2, 1)
-    V.tensor_scalar(T.offf[:], T.posf[:], float(C), None, A.mult).then_inc(sem.f3, 1)
-    V.wait_ge(sem.f3, 1)
+    for half in (lo, hi):
+        V.tensor_scalar(T.offf[half, :], T.posf[lo, :], float(C), None, A.mult).then_inc(sem.f3, 1)
+    V.wait_ge(sem.ld_w1, 16)
+    V.quantize_mx(T.wc[:, 256:512], T.wsc[:, 256:512], T.ws[:, 1024:2048]).then_inc(sem.qw1, 1)
+    V.wait_ge(sem.f3, 2)
     V.wait_ge(sem.qoo, 1)
     V.wait_ge(sem.a_oc, arr)
     V.wait_ge(sem.a_cc, far_in)
     V.tensor_copy(T.mc[:].bitcast(dt.uint32),
                   T.wino[:].bitcast(dt.uint32).indirect(T.offf[:, 0:KC])).then_inc(sem.pkfc, 1)
-    S.wait_ge(sem.f3, 1)
+    S.wait_ge(sem.f3, 2)
     S.wait_ge(sem.qoo, 1)
     S.wait_ge(sem.a_os, arr)
     S.wait_ge(sem.a_cs, far_in)
     S.activation(T.ms[:], T.winos[:].indirect(T.offf[:, 0:KC]), ActivationFunctionType.Copy).then_inc(sem.pkfs, 1)
 
-    P.wait_ge(sem.qw, 1)
+    P.wait_ge(sem.qw0, 1)
+    P.wait_ge(sem.qw1, 1)
     P.wait_ge(sem.pkfc, 1)
     P.wait_ge(sem.pkfs, 1)
     for o in range(4):
-        P.matmul_mx(T.ps[:, 512 * o:512 * o + C], T.wc[:, C * o:C * (o + 1)], T.wsc[:, C * o:C * (o + 1)],
+        P.matmul_mx(T.ps[:, 512 * o:512 * o + C], block(T.wc, o), block(T.wsc, o),
                     T.mc[:], T.ms[:], True, True).then_inc(sem["mm%d" % o], 1)
     for o in (0, 2):
         V.wait_ge(sem["mm%d" % o], 1)
-        V.tensor_copy(T.ysb[:, C * o:C * (o + 1)], T.ps[:, 512 * o:512 * o + C]).then_inc(sem["cp%d" % o], 1)
+        V.tensor_copy(block(T.ysb, o), T.ps[:, 512 * o:512 * o + C]).then_inc(sem["cp%d" % o], 1)
     for o in (1, 3):
         S.wait_ge(sem["mm%d" % o], 1)
-        S.activation(T.ysb[:, C * o:C * (o + 1)], T.ps[:, 512 * o:512 * o + C],
+        S.activation(block(T.ysb, o), T.ps[:, 512 * o:512 * o + C],
                      ActivationFunctionType.Copy).then_inc(sem["cp%d" % o], 1)
     D.wait_ge(sem.cp0, 1)
     D.wait_ge(sem.cp1, 1)
-    D.dma_start(T.y[:, 0:2 * C], T.ysb[:, 0:2 * C]).then_inc(sem.st0, 16)
+    D.dma_start(block(T.y, 0, 2), block(T.ysb, 0, 2)).then_inc(sem.st0, 16)
     S.wait_ge(sem.cp2, 1)
     S.wait_ge(sem.cp3, 1)
-    S.dma_start(T.y[:, 2 * C:4 * C], T.ysb[:, 2 * C:4 * C]).then_inc(sem.st1, 16)
+    S.dma_start(block(T.y, 2, 2), block(T.ysb, 2, 2)).then_inc(sem.st1, 16)
     D.wait_ge(sem.st0, 16)
     S.wait_ge(sem.st1, 16)
     g.wait_ge(sem.left, sent[0])

@@ -3,37 +3,36 @@ from concourse.mybir import dt, AluOpType, ActivationFunctionType
 
 C = 128
 KC = C // 16
-HALF = 64
+G = 32
+ST = 4
+W_EARLY, W_BETWEEN, W_LATE = [], [(0, 2), (2, 3)], [(3, 4)]
 
 CODE = "float8_e4m3fn_x4"
 SCRATCH = {
     "xs": ("sbuf", [128, 4096], "bfloat16"),
     "ws": ("sbuf", [128, 2048], "bfloat16"),
-    "scs": ("sbuf", [128, 64], "int32"),
-    "keys": ("sbuf", [128, 4 * KC], "int32"),
-    "keyland": ("sbuf", [128, 3 * KC], "int32"),
-    "max1": ("sbuf", [128, KC], "int32"),
-    "max2": ("sbuf", [128, KC], "int32"),
+    "scs": ("sbuf", [128, 4 * KC], "int32"),
+    "scl": ("sbuf", [128, 4, 2 * KC], "int32"),
+    "pair": ("sbuf", [128, 2, KC], "int32"),
     "best": ("sbuf", [128, KC], "int32"),
-    "xkey": ("sbuf", [128, KC], "int32"),
-    "xkeyland": ("sbuf", [128, KC], "int32"),
-    "fin": ("sbuf", [128, KC], "int32"),
+    "bestland": ("sbuf", [128, KC], "int32"),
     "pidx": ("sbuf", [128, KC], "int32"),
     "p16": ("sbuf", [128, KC], "int32"),
     "c16": ("sbuf", [128, KC], "int32"),
-    "jint": ("sbuf", [128, KC], "int32"),
-    "jfrac": ("sbuf", [128, KC], "float32"),
-    "lowx": ("sbuf", [128, KC], "int32"),
-    "posx": ("sbuf", [128, KC], "float32"),
+    "d0": ("sbuf", [128, ST * KC], "float32"),
+    "d1": ("sbuf", [128, ST * KC], "float32"),
+    "pos": ("sbuf", [128, ST * KC], "float32"),
+    "e0": ("sbuf", [128, 2 * KC], "float32"),
+    "e1": ("sbuf", [128, 2 * KC], "float32"),
+    "pv": ("sbuf", [128, 2 * KC], "float32"),
     "offx": ("sbuf", [128, KC], "uint16"),
-    "lowf": ("sbuf", [128, KC], "int32"),
-    "posf": ("sbuf", [128, KC], "float32"),
     "offf": ("sbuf", [128, KC], "uint16"),
     "qxc": ("sbuf", [128, 4 * C], CODE),
     "qxs": ("sbuf", [128, 4 * C], "uint8"),
     "qoc": ("sbuf", [128, 4 * C], CODE),
     "qos": ("sbuf", [128, 4 * C], "uint8"),
     "relc": ("sbuf", [128, 2 * C], CODE),
+    "rels": ("sbuf", [128, 2 * C], "uint8"),
     "winx": ("sbuf", [128, 4 * C], CODE),
     "winxs": ("sbuf", [128, 4 * C], "uint8"),
     "wino": ("sbuf", [128, 5 * C], CODE),
@@ -45,14 +44,17 @@ SCRATCH = {
     "wc": ("sbuf", [128, 512], CODE),
     "wsc": ("sbuf", [128, 512], "uint8"),
     "ps": ("psum", [128, 2048], "float32"),
+    "junk": ("sbuf", [128, 480], "float32"),
+    "junk2": ("sbuf", [128, 300], "float32"),
+    "rec": ("sbuf", [128, KC], "float32"),
     "ysb": ("sbuf", [128, 512], "float32"),
 }
 SEMAPHORES = [
-    "ld_xa", "ld_xn", "ld_oa", "ld_on", "ld_w0", "ld_w1", "ld_sc", "xsent",
-    "iot", "b0", "b1", "b2", "kmade", "qx", "qxo", "qoa", "qon", "qoo", "qw0", "qw1",
-    "mx12", "mx3", "lx0", "lx1", "lx2", "ck", "f0", "f1", "f2", "f3",
+    "ld_xa", "ld_xn", "ld_xo", "ld_oa", "ld_on", "ld_ob", "ld_oo", "ld_w0", "ld_w1", "ld_w2", "ld_w3", "ld_sx", "ld_so", "xsent",
+    "iot", "iot2", "b0", "b2", "b3", "b4", "zero", "const", "own", "qx", "qxn", "qxo", "qoa", "qon", "qoo", "qw0", "qw1", "qw2", "qw3",
+    "l0", "l1", "l2", "jk", "lx", "ck", "f0", "f1", "f2", "f3",
     "pkxc", "pkxs", "pkfc", "pkfs",
-    "a_key", "a_rc", "a_xc", "a_xs", "a_oc", "a_os", "a_ck", "a_cc", "a_cs", "left",
+    "qob", "a_key", "a_rc", "a_rd", "a_rs", "a_xc", "a_xs", "a_oc", "a_on", "a_os", "a_ck", "a_cc", "a_cs", "left",
     "mm0", "mm1", "mm2", "mm3", "cp0", "cp1", "cp2", "cp3", "st0", "st1",
 ]
 
@@ -70,6 +72,12 @@ def helper_of(c, cores, topo):
             if h not in cores and topo.die(h) == topo.die(c) and all(topo.may_write(h, k) for k in host)][0]
 
 
+def on_chip(src, far, topo):
+    off = topo.engines(src, far)
+    near = [k for k in topo.cores_of(src) if k != src][0]
+    return [e for e in topo.engines(src, near) if e not in off]
+
+
 def split(src, dsts, topo, wide=True):
     aw = [d for d in dsts if d not in topo.cores_of(src)]
     off = topo.engines(src, aw[0])
@@ -79,19 +87,19 @@ def split(src, dsts, topo, wide=True):
         m[d] = off[i * k:(i + 1) * k]
     for d in dsts:
         if d not in aw:
-            rest = [e for e in topo.engines(src, d) if e not in off]
+            rest = on_chip(src, aw[0], topo)
             m[d] = rest if wide else rest[::len(rest) // k]
     return m
 
 
-def fused(g, topo, core, masks, local_sem, sides):
+def fused(g, topo, core, local_sem, sides):
     tr = []
-    for d, s, src, dst in sides:
+    for d, engines, s, src, dst in sides:
         rid, pid = topo.addr(d, core)
-        tr.append(RemoteDMATransfer(dst_ids=[DstId(rid=rid, pnc=pid)], dma_engine_mask=mask_of(masks[d]),
+        tr.append(RemoteDMATransfer(dst_ids=[DstId(rid=rid, pnc=pid)], dma_engine_mask=mask_of(engines),
                                     remote_sem=s, srcs=[src], dsts=[dst]))
     g.remote_dma_fused(tr, local_sem=local_sem)
-    return sum(len(masks[d]) for d in masks)
+    return sum(len(engines) for _, engines, _, _, _ in sides)
 
 
 def u8(view):
@@ -102,10 +110,22 @@ def helper_program(g, core, boss, T, topo):
     cores = list(T.cores)
     mine = [c for c in cores if topo.host(c) == topo.host(boss)]
     away = [c for c in mine if c not in topo.cores_of(boss)]
-    ao = C * (len(mine) - 1 - mine.index(boss) + (1 if mine[0] == cores[0] else 0))
-    g.wait_ge(T.sem.a_rc, len(split(boss, away + [core], topo)[core]))
-    sent = fused(g, topo, core, split(core, away, topo), T.sem.left,
-                 [(d, T.sem.a_oc, u8(T.relc[:, C * i:C * (i + 1)]), u8(T.wino[:, ao:ao + C])) for i, d in enumerate(away)])
+    ao = C * mine.index(boss)
+    m = split(core, away, topo)
+    rest = len(on_chip(boss, away[0], topo))
+
+    def scales(i):
+        return fused(g, topo, core, T.sem.left, [(away[i], topo.engines(core, away[i]), T.sem.a_os,
+                                                  T.rels[:, C * i:C * (i + 1)], T.winos[:, ao:ao + C])])
+
+    g.wait_ge(T.sem.a_rs, rest // 2)
+    sent = scales(0)
+    g.wait_ge(T.sem.a_rc, rest)
+    sent += fused(g, topo, core, T.sem.left,
+                  [(d, m[d], T.sem.a_oc, u8(T.relc[:, C * i:C * (i + 1)]), u8(T.wino[:, ao:ao + C]))
+                   for i, d in enumerate(away)])
+    g.wait_ge(T.sem.a_rd, rest // 2)
+    sent += scales(1)
     g.wait_ge(T.sem.left, sent)
 
 
@@ -131,158 +151,202 @@ def rank_program(g, core, T, topo):
     V, S, P, D = g.vector, g.scalar, g.tensor, g.sync
     sem = T.sem
     A = AluOpType
-
-    xadd = 4 if first else 0
-    xslot = len(mine) - 1 - pos
-    oslot = xslot + (1 if first else 0)
-    ax, ao, ap = C * xslot, C * oslot, C * xadd
+    at, far_at = C * pos, C * len(mine)
 
     def but(c):
         return [k for k in host if k != c]
 
     thin = split(core, but(core), topo, False)
-    wide = split(core, but(core), topo)
-    arr_k = sum(len(split(c, but(c), topo, False)[core]) for c in but(core))
+    rest = on_chip(core, partner, topo)
+    other_half = [e for e in rest if e not in thin[host[near]]]
+    far = topo.engines(core, partner)
+    arr_thin = sum(len(split(c, but(c), topo, False)[core]) for c in but(core))
     arr = sum(len(split(c, but(c), topo)[core]) for c in but(core))
-    far_in = len(topo.engines(partner, core))
     sent = [0]
 
-    def send(masks, sides):
-        sent[0] += fused(g, topo, core, {d: masks[d] for d, _, _, _ in sides}, sem.left, sides)
+    def send(sides):
+        sent[0] += fused(g, topo, core, sem.left, sides)
 
-    def spread(masks, s, src, dst):
-        send(masks, [(host[p], s, src(p), dst(p)) for p in peers])
+    def spread(s, src, dst):
+        send([(host[p], thin[host[p]], s, src(p), dst) for p in peers])
 
     def block(buf, p, k=1):
         return buf[:, C * p:C * (p + k)]
 
-    def load_x(ranks, s):
+    def load_x(ranks, s, q=D):
         a, b = 4 * C * min(ranks), 4 * C * (max(ranks) + 1)
-        D.dma_start(T.xs[:, a:b], T.x[:, a:b]).then_inc(s, 16)
+        q.dma_start(T.xs[:, a:b], T.x[:, a:b]).then_inc(s, 16)
 
-    for k, q in enumerate((D, S)):
-        q.dma_start(T.scs[16 * k:16 * k + 16, :], T.sc[:]).then_inc(sem.ld_sc, 16)
-    load_x([mine[p] for p in away], sem.ld_oa)
+    nb = KC * len(mine)
+    for base, r0, s in ((0, others[0], sem.ld_sx), (G, mine[0], sem.ld_sx)):
+        for k, q in enumerate((D, S)):
+            a = base + 16 * k
+            q.dma_start(T.scs[a:a + 16, :], T.sc[:, KC * r0:KC * r0 + nb]).then_inc(s, 16)
     load_x([others[p] for p in away], sem.ld_xa)
-    load_x([others[near], others[pos]], sem.ld_xn)
+    load_x([others[near]], sem.ld_xn)
+    load_x([mine[away[0]]], sem.ld_oa)
+    load_x([mine[away[1]]], sem.ld_ob)
+    load_x([others[pos]], sem.ld_xo)
     load_x([mine[near], mine[pos]], sem.ld_on)
-    D.dma_start(T.ws[:, 0:1024], T.w[:, 0:1024]).then_inc(sem.ld_w0, 16)
+
+    def load_w(runs):
+        for a, b in runs:
+            D.dma_start(T.ws[:, 512 * a:512 * b], T.w[:, 512 * a:512 * b]).then_inc(sem["ld_w%d" % a], 16)
+
+    def quant_w(runs):
+        for a, b in runs:
+            V.wait_ge(sem["ld_w%d" % a], 16)
+            V.quantize_mx(block(T.wc, a, b - a), block(T.wsc, a, b - a),
+                          T.ws[:, 512 * a:512 * b]).then_inc(sem["qw%d" % a], 1)
+
+    load_w(W_EARLY)
     D.wait_ge(sem.xsent, 1)
-    D.dma_start(T.ws[:, 1024:2048], T.w[:, 1024:2048]).then_inc(sem.ld_w1, 16)
+    load_w(W_BETWEEN[:1])
+    D.wait_ge(sem.ck, 1)
+    load_w(W_BETWEEN[1:])
+    load_w(W_LATE)
+
+    lists, xl, ol = slice(0, 2 * G), slice(0, G), slice(G, 2 * G)
+
+    def step(buf, k, part=lists):
+        return buf[part, k:ST * KC:ST]
 
     g.iota(T.pidx[:], [[0, KC]], 0, 1).then_inc(sem.iot, 1)
-    g.iota(T.c16[:], [[16, KC]], 0, 0).then_inc(sem.iot, 1)
-    V.wait_ge(sem.iot, 2)
+    g.iota(T.c16[:], [[16, KC]], C, 0).then_inc(sem.iot2, 1)
+    V.memset(T.scs[2 * G:128, :], 0).then_inc(sem.zero, 1)
+    V.memset(step(T.d0, 0), 0.0).then_inc(sem.const, 1)
+    V.wait_ge(sem.iot, 1)
     V.tensor_scalar(T.p16[:], T.pidx[:], 15, None, A.bitwise_and).then_inc(sem.b0, 1)
-
-    lo, hi = slice(0, HALF), slice(HALF, 128)
-    nb = KC * len(mine)
-    V.wait_ge(sem.ld_sc, 32)
-    for a in range(0, 128, 32):
-        r0, low = (mine[0], oslot) if a < HALF else (others[0], xslot + xadd)
-        V.tensor_scalar(T.keys[a:a + 32, :], T.scs[0:32, KC * r0:KC * r0 + nb], 8.0, float(low),
-                        A.mult, A.add).then_inc(sem.kmade, 1)
-    g.wait_ge(sem.kmade, 4)
+    V.wait_ge(sem.iot2, 1)
     V.wait_ge(sem.b0, 1)
-    V.tensor_tensor(T.jint[:], T.p16[:], T.c16[:], A.add).then_inc(sem.b1, 1)
+    V.tensor_tensor(step(T.d0, 3), T.p16[lists, :], T.c16[lists, :], A.add).then_inc(sem.b3, 1)
+    V.wait_ge(sem.b3, 1)
+    V.reciprocal(T.rec[lists, :], step(T.d0, 3)).then_inc(sem.b4, 1)
+    S.wait_ge(sem.b3, 1)
+    S.activation(step(T.d1, 3), step(T.d0, 3), ActivationFunctionType.Identity, bias=float(-C)).then_inc(sem.const, 1)
+    S.activation(T.e1[ol, 0:2 * KC:2], step(T.d0, 3, ol), ActivationFunctionType.Identity,
+                 bias=float(far_at - C)).then_inc(sem.b2, 1)
+    S.activation(T.e0[ol, 0:2 * KC:2], step(T.d0, 3, ol), ActivationFunctionType.Identity, scale=0.0).then_inc(sem.b2, 1)
 
-    def lane(to):
-        return pos if pos < to else pos - 1
+    lane = 2 * (pos % 2) + pos // 2
+    h = KC * (pos - min(pos, near))
+    g.wait_ge(sem.zero, 1)
+    g.wait_ge(sem.ld_sx, 64)
+    tr = []
+    for ps, engines in ((away, far), ([near], thin[host[near]])):
+        ids = [DstId(rid=topo.addr(host[p], core)[0], pnc=topo.addr(host[p], core)[1]) for p in ps]
+        b = KC * (min(ps) if len(ps) > 1 else min(pos, near))
+        tr.append(RemoteDMATransfer(dst_ids=ids, dma_engine_mask=mask_of(engines), remote_sem=sem.a_key,
+                                    srcs=[T.scs[:, b:b + 2 * KC]], dsts=[T.scl[:, lane, :] for _ in ps]))
+        sent[0] += len(engines)
+    g.remote_dma_fused(tr, local_sem=sem.left)
+    V.wait_ge(sem.zero, 1)
+    V.wait_ge(sem.ld_sx, 64)
+    V.tensor_copy(T.scl[:, lane, h:h + KC], T.scs[:, KC * pos:KC * (pos + 1)]).then_inc(sem.own, 1)
+    S.wait_ge(sem.b4, 1)
+    for buf, k in ((T.d0, 2), (T.d1, 1)):
+        S.activation(step(buf, 1), T.rec[lists, :], ActivationFunctionType.Identity, bias=1.0,
+                     scale=float(k * C)).then_inc(sem.const, 1)
 
-    spread(thin, sem.a_key, lambda p: T.keys[:, KC * p:KC * (p + 1)],
-           lambda p: T.keyland[:, KC * lane(p):KC * (lane(p) + 1)])
-
-    def quant(codes, scales, at, ranks, p, k, s):
-        V.quantize_mx(codes[:, at:at + k * C], scales[:, at:at + k * C],
+    def quant(codes, scales, to, ranks, p, k, s):
+        V.quantize_mx(codes[:, to:to + k * C], scales[:, to:to + k * C],
                       T.xs[:, 4 * C * ranks[p]:4 * C * (ranks[p] + k)]).then_inc(s, 1)
 
     a0 = min(away)
-    V.wait_ge(sem.ld_oa, 16)
-    quant(T.qoc, T.qos, C * a0, mine, a0, len(away), sem.qoa)
-    V.wait_ge(sem.b1, 1)
-    V.tensor_scalar(T.jfrac[:], T.jint[:], 1.0 / C, None, A.mult).then_inc(sem.b2, 1)
     V.wait_ge(sem.ld_xa, 16)
     quant(T.qxc, T.qxs, C * a0, others, a0, len(away), sem.qx)
     V.wait_ge(sem.ld_xn, 16)
-    quant(T.qxc, T.qxs, C * near, others, near, 1, sem.qx)
-    quant(T.winx, T.winxs, ax, others, pos, 1, sem.qxo)
-    V.wait_ge(sem.ld_on, 16)
-    quant(T.qoc, T.qos, C * near, mine, near, 1, sem.qon)
-    quant(T.wino, T.winos, ao, mine, pos, 1, sem.qoo)
+    quant(T.qxc, T.qxs, C * near, others, near, 1, sem.qxn)
+    V.wait_ge(sem.ld_oa, 16)
+    quant(T.qoc, T.qos, C * a0, mine, a0, 1, sem.qoa)
+    V.wait_ge(sem.ld_ob, 16)
+    quant(T.qoc, T.qos, C * (a0 + 1), mine, a0 + 1, 1, sem.qob)
+    V.wait_ge(sem.ld_xo, 16)
+    quant(T.winx, T.winxs, at, others, pos, 1, sem.qxo)
 
+    g.wait_ge(sem.qx, 1)
+    g.wait_ge(sem.qxn, 1)
+    spread(sem.a_xc, lambda p: u8(block(T.qxc, p)), u8(T.winx[:, at:at + C]))
     g.wait_ge(sem.qoa, 1)
-    send({helper: wide[host[near]]}, [(helper, sem.a_rc, u8(block(T.qoc, a0, len(away))), u8(T.relc[:]))])
-    g.wait_ge(sem.qx, 2)
-    spread(wide, sem.a_xc, lambda p: u8(block(T.qxc, p)), lambda p: u8(T.winx[:, ax:ax + C]))
-    spread(wide, sem.a_xs, lambda p: block(T.qxs, p), lambda p: T.winxs[:, ax:ax + C])
-    g.wait_ge(sem.qon, 1)
-    spread(wide, sem.a_os, lambda p: block(T.qos, p), lambda p: T.winos[:, ao:ao + C])
+    send([(helper, other_half, sem.a_rs, block(T.qos, a0), block(T.rels, 0))])
+    g.wait_ge(sem.qob, 1)
+    send([(helper, rest, sem.a_rc, u8(block(T.qoc, a0, len(away))), u8(T.relc[:]))])
     g.sem_inc(sem.xsent, 1)
+    send([(host[p], thin[host[p]], sem.a_xs, block(T.qxs, p), T.winxs[:, at:at + C]) for p in peers]
+         + [(helper, other_half, sem.a_rd, block(T.qos, a0 + 1), block(T.rels, 1))])
 
-    V.wait_ge(sem.a_key, arr_k)
-    V.tensor_tensor(T.max1[:], T.keyland[:, 0:KC], T.keyland[:, KC:2 * KC], A.max).then_inc(sem.mx12, 1)
-    V.wait_ge(sem.kmade, 4)
-    V.tensor_tensor(T.max2[:], T.keyland[:, 2 * KC:3 * KC], T.keys[:, KC * pos:KC * (pos + 1)], A.max).then_inc(sem.mx12, 1)
-    V.wait_ge(sem.mx12, 2)
-    V.tensor_tensor(T.best[:], T.max1[:], T.max2[:], A.max).then_inc(sem.mx3, 1)
-    V.wait_ge(sem.mx3, 1)
-    V.tensor_scalar(T.lowx[hi, :], T.best[hi, :], 7, None, A.bitwise_and).then_inc(sem.lx0, 1)
-    V.tensor_scalar(T.xkey[:], T.best[:], 0x7FFFFFFC, None, A.bitwise_and).then_inc(sem.ck, 1)
-    V.wait_ge(sem.lx0, 1)
-    V.wait_ge(sem.b2, 1)
-    V.tensor_tensor(T.posx[hi, :], T.lowx[hi, :], T.jfrac[hi, :], A.add).then_inc(sem.lx1, 1)
-    V.wait_ge(sem.lx1, 1)
-    for half in (lo, hi):
-        V.tensor_scalar(T.offx[half, :], T.posx[hi, :], float(C), float(-C * xadd), A.mult, A.add).then_inc(sem.lx2, 1)
-    last = split(core, [partner, host[near]], topo)
+    V.wait_ge(sem.own, 1)
+    V.wait_ge(sem.a_key, 2 * len(far) + len(thin[host[near]]))
+    V.tensor_tensor(T.pair[:], T.scl[:, 0:2, h:h + KC], T.scl[:, 2:4, h:h + KC], A.max).then_inc(sem.l0, 1)
+    for k, a in ((2, 0), (0, 1)):
+        V.tensor_tensor(step(T.d1, k), T.scl[lists, 2 + a, h:h + KC], T.scl[lists, a, h:h + KC],
+                        A.is_gt).then_inc(sem.l1, 1)
+    V.wait_ge(sem.l0, 1)
+    V.tensor_tensor(step(T.d0, 2), T.pair[lists, 1, :], T.pair[lists, 0, :], A.is_gt).then_inc(sem.l1, 1)
+    V.tensor_tensor(T.best[:], T.pair[:, 1, :], T.pair[:, 0, :], A.max).then_inc(sem.ck, 1)
+    V.wait_ge(sem.l1, 3)
+    V.wait_ge(sem.const, 4)
+    V.tensor_tensor_scan(T.pos[lists, :], T.d0[lists, :], T.d1[lists, :], 0.0, A.mult, A.max).then_inc(sem.l2, 1)
+    V.wait_ge(sem.l2, 1)
+    for a in range(0, 128, G):
+        V.tensor_scalar(T.offx[a:a + G, :], step(T.pos, 3, xl), 0.25, None, A.add).then_inc(sem.lx, 1)
+    quant_w(W_EARLY)
     g.wait_ge(sem.ck, 1)
-    send(last, [(partner, sem.a_ck, T.xkey[:], T.xkeyland[:])])
+    send([(partner, far, sem.a_ck, T.best[:], T.bestland[:])])
 
-    V.wait_ge(sem.lx2, 2)
+    S.wait_ge(sem.l2, 1)
+    S.activation(T.e1[ol, 1:2 * KC:2], step(T.pos, 3, ol), ActivationFunctionType.Copy).then_inc(sem.b2, 1)
+    S.wait_ge(sem.lx, 4)
+    S.wait_ge(sem.qxo, 1)
+    S.wait_ge(sem.a_xs, arr_thin)
+    S.activation(T.sels[:], T.winxs[:].indirect(T.offx[:, 0:KC]), ActivationFunctionType.Copy).then_inc(sem.pkxs, 1)
+    V.wait_ge(sem.lx, 4)
     V.wait_ge(sem.qxo, 1)
-    V.wait_ge(sem.a_xc, arr)
+    V.wait_ge(sem.a_xc, arr_thin)
     V.tensor_copy(T.selc[:].bitcast(dt.uint32),
                   T.winx[:].bitcast(dt.uint32).indirect(T.offx[:, 0:KC])).then_inc(sem.pkxc, 1)
-    S.wait_ge(sem.lx2, 2)
-    S.wait_ge(sem.qxo, 1)
-    S.wait_ge(sem.a_xs, arr)
-    S.activation(T.sels[:], T.winxs[:].indirect(T.offx[:, 0:KC]), ActivationFunctionType.Copy).then_inc(sem.pkxs, 1)
+    V.wait_ge(sem.ld_on, 16)
+    quant(T.qoc, T.qos, C * near, mine, near, 1, sem.qon)
+    quant(T.wino, T.winos, at, mine, pos, 1, sem.qoo)
     g.wait_ge(sem.pkxc, 1)
-    send(last, [(partner, sem.a_cc, u8(T.selc[:]), u8(T.wino[:, ap:ap + C])),
-                (host[near], sem.a_oc, u8(block(T.qoc, near)), u8(T.wino[:, ao:ao + C]))])
+    send([(partner, far, sem.a_cc, u8(T.selc[:]), u8(T.wino[:, far_at:far_at + C]))])
+    g.wait_ge(sem.qon, 1)
+    send([(host[near], rest, sem.a_on, u8(block(T.qoc, near)), u8(T.wino[:, at:at + C]))])
     g.wait_ge(sem.pkxs, 1)
-    send(last, [(partner, sem.a_cs, T.sels[:], T.winos[:, ap:ap + C])])
+    send([(partner, far, sem.a_cs, T.sels[:], T.winos[:, far_at:far_at + C]),
+          (host[near], rest, sem.a_os, block(T.qos, near), T.winos[:, at:at + C])])
 
-    V.wait_ge(sem.ld_w0, 16)
-    V.quantize_mx(T.wc[:, 0:256], T.wsc[:, 0:256], T.ws[:, 0:1024]).then_inc(sem.qw0, 1)
-    V.wait_ge(sem.a_ck, far_in)
-    V.tensor_tensor(T.fin[lo, :], T.best[lo, :], T.xkeyland[hi, :], A.max).then_inc(sem.f0, 1)
+    quant_w(W_BETWEEN[:1])
+    V.wait_ge(sem.ck, 1)
+    V.wait_ge(sem.a_ck, len(far))
+    V.tensor_tensor(T.e0[ol, 1:2 * KC:2], T.bestland[0:G, :], T.best[ol, :],
+                    A.is_gt if first else A.is_ge).then_inc(sem.f0, 1)
     V.wait_ge(sem.f0, 1)
-    V.tensor_scalar(T.lowf[lo, :], T.fin[lo, :], 7, None, A.bitwise_and).then_inc(sem.f1, 1)
-    V.wait_ge(sem.f1, 1)
-    V.tensor_tensor(T.posf[lo, :], T.lowf[lo, :], T.jfrac[lo, :], A.add).then_inc(sem.f2, 1)
+    V.wait_ge(sem.b2, 3)
+    V.tensor_tensor_scan(T.pv[ol, :], T.e0[ol, :], T.e1[ol, :], 0.0, A.mult, A.max).then_inc(sem.f2, 1)
     V.wait_ge(sem.f2, 1)
-    for half in (lo, hi):
-        V.tensor_scalar(T.offf[half, :], T.posf[lo, :], float(C), None, A.mult).then_inc(sem.f3, 1)
-    V.wait_ge(sem.ld_w1, 16)
-    V.quantize_mx(T.wc[:, 256:512], T.wsc[:, 256:512], T.ws[:, 1024:2048]).then_inc(sem.qw1, 1)
-    V.wait_ge(sem.f3, 2)
+    for a in range(0, 128, G):
+        V.tensor_scalar(T.offf[a:a + G, :], T.pv[ol, 1:2 * KC:2], 0.25, None, A.add).then_inc(sem.f3, 1)
+    quant_w(W_BETWEEN[1:])
+    S.wait_ge(sem.f3, 4)
+    S.wait_ge(sem.qoo, 1)
+    S.wait_ge(sem.a_os, 2 * len(far) + len(rest))
+    S.wait_ge(sem.a_cs, len(far))
+    S.activation(T.ms[:], T.winos[:].indirect(T.offf[:, 0:KC]), ActivationFunctionType.Copy).then_inc(sem.pkfs, 1)
+    V.wait_ge(sem.f3, 4)
     V.wait_ge(sem.qoo, 1)
-    V.wait_ge(sem.a_oc, arr)
-    V.wait_ge(sem.a_cc, far_in)
+    V.wait_ge(sem.a_oc, arr - len(rest))
+    V.wait_ge(sem.a_on, len(rest))
+    V.wait_ge(sem.a_cc, len(far))
     V.tensor_copy(T.mc[:].bitcast(dt.uint32),
                   T.wino[:].bitcast(dt.uint32).indirect(T.offf[:, 0:KC])).then_inc(sem.pkfc, 1)
-    S.wait_ge(sem.f3, 2)
-    S.wait_ge(sem.qoo, 1)
-    S.wait_ge(sem.a_os, arr)
-    S.wait_ge(sem.a_cs, far_in)
-    S.activation(T.ms[:], T.winos[:].indirect(T.offf[:, 0:KC]), ActivationFunctionType.Copy).then_inc(sem.pkfs, 1)
 
-    P.wait_ge(sem.qw0, 1)
-    P.wait_ge(sem.qw1, 1)
+    quant_w(W_LATE)
     P.wait_ge(sem.pkfc, 1)
     P.wait_ge(sem.pkfs, 1)
     for o in range(4):
+        if o in [a for a, _ in W_EARLY + W_BETWEEN + W_LATE]:
+            P.wait_ge(sem["qw%d" % o], 1)
         P.matmul_mx(T.ps[:, 512 * o:512 * o + C], block(T.wc, o), block(T.wsc, o),
                     T.mc[:], T.ms[:], True, True).then_inc(sem["mm%d" % o], 1)
     for o in (0, 2):
@@ -293,11 +357,12 @@ def rank_program(g, core, T, topo):
         S.activation(block(T.ysb, o), T.ps[:, 512 * o:512 * o + C],
                      ActivationFunctionType.Copy).then_inc(sem["cp%d" % o], 1)
     D.wait_ge(sem.cp0, 1)
+    D.dma_start(block(T.y, 0), block(T.ysb, 0)).then_inc(sem.st0, 16)
     D.wait_ge(sem.cp1, 1)
-    D.dma_start(block(T.y, 0, 2), block(T.ysb, 0, 2)).then_inc(sem.st0, 16)
+    D.dma_start(block(T.y, 1), block(T.ysb, 1)).then_inc(sem.st0, 16)
     S.wait_ge(sem.cp2, 1)
     S.wait_ge(sem.cp3, 1)
     S.dma_start(block(T.y, 2, 2), block(T.ysb, 2, 2)).then_inc(sem.st1, 16)
-    D.wait_ge(sem.st0, 16)
+    D.wait_ge(sem.st0, 32)
     S.wait_ge(sem.st1, 16)
     g.wait_ge(sem.left, sent[0])

from concourse.bass import DstId, RemoteDMATransfer
from concourse.mybir import dt, AluOpType, ActivationFunctionType

C = 128
KC = C // 16
G = 32
ST = 4
W_EARLY, W_BETWEEN, W_LATE = [], [(0, 2), (2, 3)], [(3, 4)]

CODE = "float8_e4m3fn_x4"
SCRATCH = {
    "xs": ("sbuf", [128, 4096], "bfloat16"),
    "ws": ("sbuf", [128, 2048], "bfloat16"),
    "scs": ("sbuf", [128, 4 * KC], "int32"),
    "scl": ("sbuf", [128, 4, 2 * KC], "int32"),
    "pair": ("sbuf", [128, 2, KC], "int32"),
    "best": ("sbuf", [128, KC], "int32"),
    "bestland": ("sbuf", [128, KC], "int32"),
    "pidx": ("sbuf", [128, KC], "int32"),
    "p16": ("sbuf", [128, KC], "int32"),
    "c16": ("sbuf", [128, KC], "int32"),
    "d0": ("sbuf", [128, ST * KC], "float32"),
    "d1": ("sbuf", [128, ST * KC], "float32"),
    "pos": ("sbuf", [128, ST * KC], "float32"),
    "e0": ("sbuf", [128, 2 * KC], "float32"),
    "e1": ("sbuf", [128, 2 * KC], "float32"),
    "pv": ("sbuf", [128, 2 * KC], "float32"),
    "offx": ("sbuf", [128, KC], "uint16"),
    "offf": ("sbuf", [128, KC], "uint16"),
    "qxc": ("sbuf", [128, 4 * C], CODE),
    "qxs": ("sbuf", [128, 4 * C], "uint8"),
    "qoc": ("sbuf", [128, 4 * C], CODE),
    "qos": ("sbuf", [128, 4 * C], "uint8"),
    "relc": ("sbuf", [128, 2 * C], CODE),
    "rels": ("sbuf", [128, 2 * C], "uint8"),
    "winx": ("sbuf", [128, 4 * C], CODE),
    "winxs": ("sbuf", [128, 4 * C], "uint8"),
    "wino": ("sbuf", [128, 5 * C], CODE),
    "winos": ("sbuf", [128, 5 * C], "uint8"),
    "selc": ("sbuf", [128, C], CODE),
    "sels": ("sbuf", [128, C], "uint8"),
    "mc": ("sbuf", [128, C], CODE),
    "ms": ("sbuf", [128, C], "uint8"),
    "wc": ("sbuf", [128, 512], CODE),
    "wsc": ("sbuf", [128, 512], "uint8"),
    "ps": ("psum", [128, 2048], "float32"),
    "junk": ("sbuf", [128, 480], "float32"),
    "junk2": ("sbuf", [128, 300], "float32"),
    "rec": ("sbuf", [128, KC], "float32"),
    "ysb": ("sbuf", [128, 512], "float32"),
}
SEMAPHORES = [
    "ld_xa", "ld_xn", "ld_xo", "ld_oa", "ld_on", "ld_ob", "ld_oo", "ld_w0", "ld_w1", "ld_w2", "ld_w3", "ld_sx", "ld_so", "xsent",
    "iot", "iot2", "b0", "b2", "b3", "b4", "zero", "const", "own", "qx", "qxn", "qxo", "qoa", "qon", "qoo", "qw0", "qw1", "qw2", "qw3",
    "l0", "l1", "l2", "jk", "lx", "ck", "f0", "f1", "f2", "f3",
    "pkxc", "pkxs", "pkfc", "pkfs",
    "qob", "a_key", "a_rc", "a_rd", "a_rs", "a_xc", "a_xs", "a_oc", "a_on", "a_os", "a_ck", "a_cc", "a_cs", "left",
    "mm0", "mm1", "mm2", "mm3", "cp0", "cp1", "cp2", "cp3", "st0", "st1",
]


def mask_of(engines):
    m = 0
    for e in engines:
        m |= 1 << e
    return m


def helper_of(c, cores, topo):
    host = [k for k in cores if topo.host(k) == topo.host(c)]
    return [h for h in topo.cores_of(c)
            if h not in cores and topo.die(h) == topo.die(c) and all(topo.may_write(h, k) for k in host)][0]


def on_chip(src, far, topo):
    off = topo.engines(src, far)
    near = [k for k in topo.cores_of(src) if k != src][0]
    return [e for e in topo.engines(src, near) if e not in off]


def split(src, dsts, topo, wide=True):
    aw = [d for d in dsts if d not in topo.cores_of(src)]
    off = topo.engines(src, aw[0])
    k = len(off) // len(aw)
    m = {}
    for i, d in enumerate(aw):
        m[d] = off[i * k:(i + 1) * k]
    for d in dsts:
        if d not in aw:
            rest = on_chip(src, aw[0], topo)
            m[d] = rest if wide else rest[::len(rest) // k]
    return m


def fused(g, topo, core, local_sem, sides):
    tr = []
    for d, engines, s, src, dst in sides:
        rid, pid = topo.addr(d, core)
        tr.append(RemoteDMATransfer(dst_ids=[DstId(rid=rid, pnc=pid)], dma_engine_mask=mask_of(engines),
                                    remote_sem=s, srcs=[src], dsts=[dst]))
    g.remote_dma_fused(tr, local_sem=local_sem)
    return sum(len(engines) for _, engines, _, _, _ in sides)


def u8(view):
    return view.bitcast(dt.uint8)


def helper_program(g, core, boss, T, topo):
    cores = list(T.cores)
    mine = [c for c in cores if topo.host(c) == topo.host(boss)]
    away = [c for c in mine if c not in topo.cores_of(boss)]
    ao = C * mine.index(boss)
    m = split(core, away, topo)
    rest = len(on_chip(boss, away[0], topo))

    def scales(i):
        return fused(g, topo, core, T.sem.left, [(away[i], topo.engines(core, away[i]), T.sem.a_os,
                                                  T.rels[:, C * i:C * (i + 1)], T.winos[:, ao:ao + C])])

    g.wait_ge(T.sem.a_rs, rest // 2)
    sent = scales(0)
    g.wait_ge(T.sem.a_rc, rest)
    sent += fused(g, topo, core, T.sem.left,
                  [(d, m[d], T.sem.a_oc, u8(T.relc[:, C * i:C * (i + 1)]), u8(T.wino[:, ao:ao + C]))
                   for i, d in enumerate(away)])
    g.wait_ge(T.sem.a_rd, rest // 2)
    sent += scales(1)
    g.wait_ge(T.sem.left, sent)


def rank_program(g, core, T, topo):
    rank = T.rank_of(core)
    cores = list(T.cores)
    if rank is None:
        for c in cores:
            if helper_of(c, cores, topo) == core:
                helper_program(g, core, c, T, topo)
        return
    n = len(cores)
    mine = [r for r in range(n) if topo.host(cores[r]) == topo.host(core)]
    others = [r for r in range(n) if r not in mine]
    pos = mine.index(rank)
    partner = cores[others[pos]]
    first = mine[0] < others[0]
    peers = [p for p in range(len(mine)) if p != pos]
    away = [p for p in peers if topo.chip(cores[mine[p]]) != topo.chip(core)]
    near = [p for p in peers if p not in away][0]
    host = [cores[r] for r in mine]
    helper = helper_of(core, cores, topo)
    V, S, P, D = g.vector, g.scalar, g.tensor, g.sync
    sem = T.sem
    A = AluOpType
    at, far_at = C * pos, C * len(mine)

    def but(c):
        return [k for k in host if k != c]

    thin = split(core, but(core), topo, False)
    rest = on_chip(core, partner, topo)
    other_half = [e for e in rest if e not in thin[host[near]]]
    far = topo.engines(core, partner)
    arr_thin = sum(len(split(c, but(c), topo, False)[core]) for c in but(core))
    arr = sum(len(split(c, but(c), topo)[core]) for c in but(core))
    sent = [0]

    def send(sides):
        sent[0] += fused(g, topo, core, sem.left, sides)

    def spread(s, src, dst):
        send([(host[p], thin[host[p]], s, src(p), dst) for p in peers])

    def block(buf, p, k=1):
        return buf[:, C * p:C * (p + k)]

    def load_x(ranks, s, q=D):
        a, b = 4 * C * min(ranks), 4 * C * (max(ranks) + 1)
        q.dma_start(T.xs[:, a:b], T.x[:, a:b]).then_inc(s, 16)

    nb = KC * len(mine)
    for base, r0, s in ((0, others[0], sem.ld_sx), (G, mine[0], sem.ld_sx)):
        for k, q in enumerate((D, S)):
            a = base + 16 * k
            q.dma_start(T.scs[a:a + 16, :], T.sc[:, KC * r0:KC * r0 + nb]).then_inc(s, 16)
    load_x([others[p] for p in away], sem.ld_xa)
    load_x([others[near]], sem.ld_xn)
    load_x([mine[away[0]]], sem.ld_oa)
    load_x([mine[away[1]]], sem.ld_ob)
    load_x([others[pos]], sem.ld_xo)
    load_x([mine[near], mine[pos]], sem.ld_on)

    def load_w(runs):
        for a, b in runs:
            D.dma_start(T.ws[:, 512 * a:512 * b], T.w[:, 512 * a:512 * b]).then_inc(sem["ld_w%d" % a], 16)

    def quant_w(runs):
        for a, b in runs:
            V.wait_ge(sem["ld_w%d" % a], 16)
            V.quantize_mx(block(T.wc, a, b - a), block(T.wsc, a, b - a),
                          T.ws[:, 512 * a:512 * b]).then_inc(sem["qw%d" % a], 1)

    load_w(W_EARLY)
    D.wait_ge(sem.xsent, 1)
    load_w(W_BETWEEN[:1])
    D.wait_ge(sem.ck, 1)
    load_w(W_BETWEEN[1:])
    load_w(W_LATE)

    lists, xl, ol = slice(0, 2 * G), slice(0, G), slice(G, 2 * G)

    def step(buf, k, part=lists):
        return buf[part, k:ST * KC:ST]

    g.iota(T.pidx[:], [[0, KC]], 0, 1).then_inc(sem.iot, 1)
    g.iota(T.c16[:], [[16, KC]], C, 0).then_inc(sem.iot2, 1)
    V.memset(T.scs[2 * G:128, :], 0).then_inc(sem.zero, 1)
    V.memset(step(T.d0, 0), 0.0).then_inc(sem.const, 1)
    V.wait_ge(sem.iot, 1)
    V.tensor_scalar(T.p16[:], T.pidx[:], 15, None, A.bitwise_and).then_inc(sem.b0, 1)
    V.wait_ge(sem.iot2, 1)
    V.wait_ge(sem.b0, 1)
    V.tensor_tensor(step(T.d0, 3), T.p16[lists, :], T.c16[lists, :], A.add).then_inc(sem.b3, 1)
    V.wait_ge(sem.b3, 1)
    V.reciprocal(T.rec[lists, :], step(T.d0, 3)).then_inc(sem.b4, 1)
    S.wait_ge(sem.b3, 1)
    S.activation(step(T.d1, 3), step(T.d0, 3), ActivationFunctionType.Identity, bias=float(-C)).then_inc(sem.const, 1)
    S.activation(T.e1[ol, 0:2 * KC:2], step(T.d0, 3, ol), ActivationFunctionType.Identity,
                 bias=float(far_at - C)).then_inc(sem.b2, 1)
    S.activation(T.e0[ol, 0:2 * KC:2], step(T.d0, 3, ol), ActivationFunctionType.Identity, scale=0.0).then_inc(sem.b2, 1)

    lane = 2 * (pos % 2) + pos // 2
    h = KC * (pos - min(pos, near))
    g.wait_ge(sem.zero, 1)
    g.wait_ge(sem.ld_sx, 64)
    tr = []
    for ps, engines in ((away, far), ([near], thin[host[near]])):
        ids = [DstId(rid=topo.addr(host[p], core)[0], pnc=topo.addr(host[p], core)[1]) for p in ps]
        b = KC * (min(ps) if len(ps) > 1 else min(pos, near))
        tr.append(RemoteDMATransfer(dst_ids=ids, dma_engine_mask=mask_of(engines), remote_sem=sem.a_key,
                                    srcs=[T.scs[:, b:b + 2 * KC]], dsts=[T.scl[:, lane, :] for _ in ps]))
        sent[0] += len(engines)
    g.remote_dma_fused(tr, local_sem=sem.left)
    V.wait_ge(sem.zero, 1)
    V.wait_ge(sem.ld_sx, 64)
    V.tensor_copy(T.scl[:, lane, h:h + KC], T.scs[:, KC * pos:KC * (pos + 1)]).then_inc(sem.own, 1)
    S.wait_ge(sem.b4, 1)
    for buf, k in ((T.d0, 2), (T.d1, 1)):
        S.activation(step(buf, 1), T.rec[lists, :], ActivationFunctionType.Identity, bias=1.0,
                     scale=float(k * C)).then_inc(sem.const, 1)

    def quant(codes, scales, to, ranks, p, k, s):
        V.quantize_mx(codes[:, to:to + k * C], scales[:, to:to + k * C],
                      T.xs[:, 4 * C * ranks[p]:4 * C * (ranks[p] + k)]).then_inc(s, 1)

    a0 = min(away)
    V.wait_ge(sem.ld_xa, 16)
    quant(T.qxc, T.qxs, C * a0, others, a0, len(away), sem.qx)
    V.wait_ge(sem.ld_xn, 16)
    quant(T.qxc, T.qxs, C * near, others, near, 1, sem.qxn)
    V.wait_ge(sem.ld_oa, 16)
    quant(T.qoc, T.qos, C * a0, mine, a0, 1, sem.qoa)
    V.wait_ge(sem.ld_ob, 16)
    quant(T.qoc, T.qos, C * (a0 + 1), mine, a0 + 1, 1, sem.qob)
    V.wait_ge(sem.ld_xo, 16)
    quant(T.winx, T.winxs, at, others, pos, 1, sem.qxo)

    g.wait_ge(sem.qx, 1)
    g.wait_ge(sem.qxn, 1)
    spread(sem.a_xc, lambda p: u8(block(T.qxc, p)), u8(T.winx[:, at:at + C]))
    g.wait_ge(sem.qoa, 1)
    send([(helper, other_half, sem.a_rs, block(T.qos, a0), block(T.rels, 0))])
    g.wait_ge(sem.qob, 1)
    send([(helper, rest, sem.a_rc, u8(block(T.qoc, a0, len(away))), u8(T.relc[:]))])
    g.sem_inc(sem.xsent, 1)
    send([(host[p], thin[host[p]], sem.a_xs, block(T.qxs, p), T.winxs[:, at:at + C]) for p in peers]
         + [(helper, other_half, sem.a_rd, block(T.qos, a0 + 1), block(T.rels, 1))])

    V.wait_ge(sem.own, 1)
    V.wait_ge(sem.a_key, 2 * len(far) + len(thin[host[near]]))
    V.tensor_tensor(T.pair[:], T.scl[:, 0:2, h:h + KC], T.scl[:, 2:4, h:h + KC], A.max).then_inc(sem.l0, 1)
    for k, a in ((2, 0), (0, 1)):
        V.tensor_tensor(step(T.d1, k), T.scl[lists, 2 + a, h:h + KC], T.scl[lists, a, h:h + KC],
                        A.is_gt).then_inc(sem.l1, 1)
    V.wait_ge(sem.l0, 1)
    V.tensor_tensor(step(T.d0, 2), T.pair[lists, 1, :], T.pair[lists, 0, :], A.is_gt).then_inc(sem.l1, 1)
    V.tensor_tensor(T.best[:], T.pair[:, 1, :], T.pair[:, 0, :], A.max).then_inc(sem.ck, 1)
    V.wait_ge(sem.l1, 3)
    V.wait_ge(sem.const, 4)
    V.tensor_tensor_scan(T.pos[lists, :], T.d0[lists, :], T.d1[lists, :], 0.0, A.mult, A.max).then_inc(sem.l2, 1)
    V.wait_ge(sem.l2, 1)
    for a in range(0, 128, G):
        V.tensor_scalar(T.offx[a:a + G, :], step(T.pos, 3, xl), 0.25, None, A.add).then_inc(sem.lx, 1)
    quant_w(W_EARLY)
    g.wait_ge(sem.ck, 1)
    send([(partner, far, sem.a_ck, T.best[:], T.bestland[:])])

    S.wait_ge(sem.l2, 1)
    S.activation(T.e1[ol, 1:2 * KC:2], step(T.pos, 3, ol), ActivationFunctionType.Copy).then_inc(sem.b2, 1)
    S.wait_ge(sem.lx, 4)
    S.wait_ge(sem.qxo, 1)
    S.wait_ge(sem.a_xs, arr_thin)
    S.activation(T.sels[:], T.winxs[:].indirect(T.offx[:, 0:KC]), ActivationFunctionType.Copy).then_inc(sem.pkxs, 1)
    V.wait_ge(sem.lx, 4)
    V.wait_ge(sem.qxo, 1)
    V.wait_ge(sem.a_xc, arr_thin)
    V.tensor_copy(T.selc[:].bitcast(dt.uint32),
                  T.winx[:].bitcast(dt.uint32).indirect(T.offx[:, 0:KC])).then_inc(sem.pkxc, 1)
    V.wait_ge(sem.ld_on, 16)
    quant(T.qoc, T.qos, C * near, mine, near, 1, sem.qon)
    quant(T.wino, T.winos, at, mine, pos, 1, sem.qoo)
    g.wait_ge(sem.pkxc, 1)
    send([(partner, far, sem.a_cc, u8(T.selc[:]), u8(T.wino[:, far_at:far_at + C]))])
    g.wait_ge(sem.qon, 1)
    send([(host[near], rest, sem.a_on, u8(block(T.qoc, near)), u8(T.wino[:, at:at + C]))])
    g.wait_ge(sem.pkxs, 1)
    send([(partner, far, sem.a_cs, T.sels[:], T.winos[:, far_at:far_at + C]),
          (host[near], rest, sem.a_os, block(T.qos, near), T.winos[:, at:at + C])])

    quant_w(W_BETWEEN[:1])
    V.wait_ge(sem.ck, 1)
    V.wait_ge(sem.a_ck, len(far))
    V.tensor_tensor(T.e0[ol, 1:2 * KC:2], T.bestland[0:G, :], T.best[ol, :],
                    A.is_gt if first else A.is_ge).then_inc(sem.f0, 1)
    V.wait_ge(sem.f0, 1)
    V.wait_ge(sem.b2, 3)
    V.tensor_tensor_scan(T.pv[ol, :], T.e0[ol, :], T.e1[ol, :], 0.0, A.mult, A.max).then_inc(sem.f2, 1)
    V.wait_ge(sem.f2, 1)
    for a in range(0, 128, G):
        V.tensor_scalar(T.offf[a:a + G, :], T.pv[ol, 1:2 * KC:2], 0.25, None, A.add).then_inc(sem.f3, 1)
    quant_w(W_BETWEEN[1:])
    S.wait_ge(sem.f3, 4)
    S.wait_ge(sem.qoo, 1)
    S.wait_ge(sem.a_os, 2 * len(far) + len(rest))
    S.wait_ge(sem.a_cs, len(far))
    S.activation(T.ms[:], T.winos[:].indirect(T.offf[:, 0:KC]), ActivationFunctionType.Copy).then_inc(sem.pkfs, 1)
    V.wait_ge(sem.f3, 4)
    V.wait_ge(sem.qoo, 1)
    V.wait_ge(sem.a_oc, arr - len(rest))
    V.wait_ge(sem.a_on, len(rest))
    V.wait_ge(sem.a_cc, len(far))
    V.tensor_copy(T.mc[:].bitcast(dt.uint32),
                  T.wino[:].bitcast(dt.uint32).indirect(T.offf[:, 0:KC])).then_inc(sem.pkfc, 1)

    quant_w(W_LATE)
    P.wait_ge(sem.pkfc, 1)
    P.wait_ge(sem.pkfs, 1)
    for o in range(4):
        if o in [a for a, _ in W_EARLY + W_BETWEEN + W_LATE]:
            P.wait_ge(sem["qw%d" % o], 1)
        P.matmul_mx(T.ps[:, 512 * o:512 * o + C], block(T.wc, o), block(T.wsc, o),
                    T.mc[:], T.ms[:], True, True).then_inc(sem["mm%d" % o], 1)
    for o in (0, 2):
        V.wait_ge(sem["mm%d" % o], 1)
        V.tensor_copy(block(T.ysb, o), T.ps[:, 512 * o:512 * o + C]).then_inc(sem["cp%d" % o], 1)
    for o in (1, 3):
        S.wait_ge(sem["mm%d" % o], 1)
        S.activation(block(T.ysb, o), T.ps[:, 512 * o:512 * o + C],
                     ActivationFunctionType.Copy).then_inc(sem["cp%d" % o], 1)
    D.wait_ge(sem.cp0, 1)
    D.dma_start(block(T.y, 0), block(T.ysb, 0)).then_inc(sem.st0, 16)
    D.wait_ge(sem.cp1, 1)
    D.dma_start(block(T.y, 1), block(T.ysb, 1)).then_inc(sem.st0, 16)
    S.wait_ge(sem.cp2, 1)
    S.wait_ge(sem.cp3, 1)
    S.dma_start(block(T.y, 2, 2), block(T.ysb, 2, 2)).then_inc(sem.st1, 16)
    D.wait_ge(sem.st0, 32)
    S.wait_ge(sem.st1, 16)
    g.wait_ge(sem.left, sent[0])
